import numpy as np
import ml_dtypes


def mxq(x, axis, fmt="e4m3"):
    dtype, down = {"e4m3": (ml_dtypes.float8_e4m3fn, 7), "e5m2": (ml_dtypes.float8_e5m2, 14)}[fmt]
    v = np.moveaxis(np.asarray(x, np.float32).astype(ml_dtypes.bfloat16).astype(np.float64), axis, -1)
    blocks = v.reshape(v.shape[:-1] + (-1, 32))
    amax = np.abs(blocks).max(-1, keepdims=True)
    byte = np.maximum(np.where(amax > 0, np.frexp(amax)[1] - 1 + 127, 0) - down, 1)
    scale = np.exp2(byte - 127.0)
    codes = (blocks / scale).astype(np.float32).astype(dtype).astype(np.float64)
    return np.moveaxis((codes * scale).reshape(v.shape), -1, axis)


WIDE = False


def mx_kscale(k):
    if not WIDE:
        return np.ones(k)
    levels = np.array([30, -30])
    if k % 512:
        return np.exp2(np.random.permutation(np.resize(levels, k // 32))).repeat(32)
    a = np.empty((k // 512, 16))
    for p in range(k // 512):
        a[p, :8] = np.random.permutation(np.resize(levels, 8))
        for g in range(8):
            far = levels[np.abs(levels - a[p, g]) >= 10]
            a[p, g + 8] = far[np.random.randint(len(far))]
    return np.exp2(a.ravel()).repeat(32)


def f64(x):
    return np.asarray(x).astype(np.float64)


def striped(idx):
    return np.tile(np.asarray(idx).reshape(-1, 16).T, (8, 1)).astype(np.uint16)


def unstriped(offs):
    return offs[:16].T.reshape(-1).astype(np.int64)


E2M1 = np.array([0.0, 0.5, 1.0, 1.5, 2.0, 3.0, 4.0, 6.0, -0.0, -0.5, -1.0, -1.5, -2.0, -3.0, -4.0, -6.0])


def pack_weight(w, fmt):
    k, n = w.shape
    w = f64(np.asarray(w, np.float32).astype(ml_dtypes.bfloat16)).reshape(k // 32, 32, n)
    amax = np.abs(w).max(1)
    if fmt in ("e4m3", "e5m2"):
        byte = np.frexp(amax)[1] - 1 + 127 - (7 if fmt == "e4m3" else 14)
    else:
        mant, ex = np.frexp(amax / 6.0)
        byte = np.where(mant > 0.5, ex, ex - 1) + 127
    byte = np.clip(np.where(amax > 0, byte, 1), 1, 254)
    scaled = (w * np.exp2(127.0 - byte)[:, None, :]).reshape(k, n).astype(np.float32)
    by_word = np.ascontiguousarray(scaled.reshape(k // 512, 128, 4, n).transpose(0, 1, 3, 2))
    if fmt in ("e4m3", "e5m2"):
        words = by_word.astype(ml_dtypes.float8_e4m3fn if fmt == "e4m3" else ml_dtypes.float8_e5m2).view(np.uint8)
    else:
        c = by_word.astype(ml_dtypes.float4_e2m1fn).view(np.uint8) & 0xF
        words = (c[..., 0::2] | (c[..., 1::2] << 4)).reshape(k // 512, 128, 2 * n)
    return np.ascontiguousarray(words), np.ascontiguousarray(byte.astype(np.uint8).reshape(k // 512, 16, n))


def unpack_weight(words, scales, fmt):
    g, _, n = scales.shape
    words = np.ascontiguousarray(words).reshape(g, 128, n, -1)
    if fmt in ("e4m3", "e5m2"):
        vals = words.view(ml_dtypes.float8_e4m3fn if fmt == "e4m3" else ml_dtypes.float8_e5m2).astype(np.float64)
    else:
        nib = np.empty((g, 128, n, 4), np.uint8)
        nib[..., 0::2] = words & 0xF
        nib[..., 1::2] = words >> 4
        vals = E2M1[nib]
    vals = vals * np.repeat(np.exp2(scales.astype(np.float64) - 127.0), 8, axis=1)[..., None]
    return vals.transpose(0, 1, 3, 2).reshape(g * 512, n)


K, T, J, R, N, S = 512, 1024, 256, 512, 256, 1024


def setup_inputs():
    n = np.random.standard_normal
    idx = np.random.permutation(T)[:J]
    idx2 = np.random.permutation(J)[:J]
    idx3 = np.random.permutation(J)[:J]
    idx4 = np.random.permutation(S)[:N]
    fk = mx_kscale(K)
    fr = mx_kscale(R)
    xtp = pack_weight(n((K, T)) / fk[:, None], "e2m1")
    wp = pack_weight(n((K, R)) * 1 / np.sqrt(K) * fk[:, None] * fr, "e5m2")
    w2p = pack_weight(n((K, R)) * 1 / np.sqrt(K) * fk[:, None] * fr, "e4m3")
    vsp = pack_weight(n((R, S)) * 1 / np.sqrt(R) / fr[:, None], "e4m3")
    return {
        "xt_words": xtp[0],
        "xt_scales": xtp[1],
        "w_words": wp[0],
        "w_scales": wp[1],
        "w2_words": w2p[0],
        "w2_scales": w2p[1],
        "sa": (np.random.uniform(0.5, 1.6, (R, 1))).astype(np.float32),
        "sb": (np.random.uniform(0.5, 1.6, (R, 1))).astype(np.float32),
        "vs_words": vsp[0],
        "vs_scales": vsp[1],
        "offs": striped(idx),
        "offs2": striped(idx2),
        "offs3": striped(idx3),
        "offs4": striped(idx4),
    }


def reference(xt_words, xt_scales, w_words, w_scales, w2_words, w2_scales, sa, sb, vs_words, vs_scales, offs, offs2, offs3, offs4):
    idx = unstriped(offs)
    idx2 = unstriped(offs2)
    idx3 = unstriped(offs3)
    idx4 = unstriped(offs4)
    xtu = unpack_weight(xt_words, xt_scales, "e2m1")
    wu = unpack_weight(w_words, w_scales, "e5m2")
    w2u = unpack_weight(w2_words, w2_scales, "e4m3")
    vsu = unpack_weight(vs_words, vs_scales, "e4m3")
    xtidxg = xtu[:, idx]
    a = wu.T @ xtidxg
    b = w2u.T @ xtidxg
    hid = np.maximum(a - b[:, idx2] * f64(sa), b - a[:, idx3] * f64(sb))
    vsidx4g = vsu[:, idx4]
    hidq = mxq(hid, 0, "e5m2")
    y = vsidx4g.T @ hidq
    return y

@@ -1,0 +1,180 @@
+from contextlib import ExitStack
+
+import concourse.mybir as mybir
+
+K, T, J, R, N, S = 512, 1024, 256, 512, 256, 1024
+FLOPS = 2 * 2 * K * R * J + 2 * R * N * J
+
+F32 = mybir.dt.float32
+BF16 = mybir.dt.bfloat16
+I32 = mybir.dt.int32
+U32 = mybir.dt.uint32
+U16 = mybir.dt.uint16
+U8 = mybir.dt.uint8
+E4M3 = mybir.dt.float8_e4m3fn_x4
+E5M2 = mybir.dt.float8_e5m2_x4
+E2M1 = mybir.dt.float4_e2m1fn_x4
+COPY = mybir.ActivationFunctionType.Copy
+SUB = mybir.AluOpType.subtract
+MAX = mybir.AluOpType.max
+
+P = 128
+PACK = 4
+HALF = J // 2
+LIST_COLS = J // 16
+
+
+def tile_list_mutualweighed_twow_store_plain_kernel(
+    tc, xt_words, xt_scales, w_words, w_scales, w2_words, w2_scales, sa, sb, vs_words, vs_scales,
+    offs, offs2, offs3, offs4, out,
+):
+    nc = tc.nc
+    with ExitStack() as ctx:
+        pool = ctx.enter_context(tc.tile_pool(name="held", bufs=1))
+        psum = ctx.enter_context(tc.psum_pool(name="psum", bufs=1))
+
+        def sb_tile(name, shape, dtype):
+            return pool.tile(shape, dtype, name=name, align_bytes=64)
+
+        def packed(words):
+            return words[0].rearrange("p n t -> p (n t)").bitcast(I32)
+
+        def load_two(queue, tile, scales):
+            rows = scales[0].bitcast(I32).rearrange("(u v r) c -> v r u c", u=2, v=2)
+            for v in range(2):
+                queue.dma_start(tile[32 * v : 32 * v + 4].bitcast(I32), rows[v])
+
+        def load_four(queue, tile, scales):
+            rows = scales[0].bitcast(I32)
+            for q in range(4):
+                queue.dma_start(tile[32 * q : 32 * q + 4, :].bitcast(I32), rows[4 * q : 4 * q + 4, :])
+
+        l1 = sb_tile("l1", [P, LIST_COLS], U16)
+        l2 = sb_tile("l2", [P, LIST_COLS], U16)
+        l3 = sb_tile("l3", [P, LIST_COLS], U16)
+        l4 = sb_tile("l4", [P, LIST_COLS], U16)
+        xw = sb_tile("xw", [P, T], U16)
+        xs2 = sb_tile("xs2", [P, 2, T], U8)
+        xs = sb_tile("xs", [P, T], U8)
+        ww = sb_tile("ww", [P, R], U32)
+        ws = sb_tile("ws", [P, R], U8)
+        w2w = sb_tile("w2w", [P, R], U32)
+        w2s = sb_tile("w2s", [P, 2, R], U8)
+        vw = sb_tile("vw", [P, S], U32)
+        vs = sb_tile("vs", [P, S], U8)
+        sa_t = sb_tile("sa_t", [P, PACK], F32)
+        sb_t = sb_tile("sb_t", [P, PACK], F32)
+
+        nc.vector.memset(w2s[0:64].bitcast(I32), 0)
+        nc.vector.memset(xs2[0:64, 0, :].bitcast(I32), 0)
+        nc.gpsimd.memset(xs2[0:64, 1, :].bitcast(I32), 0)
+        nc.gpsimd.memset(ws[:].bitcast(I32), 0)
+        nc.gpsimd.memset(vs[:].bitcast(I32), 0)
+
+        nc.sync.dma_start(l1[:], offs)
+        nc.scalar.dma_start(xw[:].bitcast(I32), xt_words[0].bitcast(I32))
+        load_two(nc.sync, w2s, w2_scales)
+        load_two(nc.sync, xs2, xt_scales)
+        nc.sync.dma_start(w2w[:].bitcast(I32), packed(w2_words))
+        nc.sync.dma_start(ww[:].bitcast(I32), packed(w_words))
+        nc.gpsimd.dma_start(sa_t[:], sa.rearrange("(p t) o -> p (t o)", t=PACK))
+        nc.sync.dma_start(l2[:], offs2)
+        load_four(nc.sync, ws, w_scales)
+        nc.sync.dma_start(vw[:].bitcast(I32), packed(vs_words))
+        nc.sync.dma_start(l4[:], offs4)
+        load_four(nc.sync, vs, vs_scales)
+        nc.sync.dma_start(sb_t[:], sb.rearrange("(p t) o -> p (t o)", t=PACK))
+        nc.sync.dma_start(l3[:], offs3)
+
+        nc.vector.tensor_copy(xs[0:64, :].bitcast(I32), xs2[0:64, 0, :].bitcast(I32))
+        nc.vector.tensor_copy(xs[64:128, :].bitcast(I32), xs2[0:64, 1, :].bitcast(I32))
+        nc.vector.tensor_copy(w2s[64:128, 0, :].bitcast(I32), w2s[0:64, 1, :].bitcast(I32))
+        xgs = sb_tile("xgs", [P, J], U8)
+        xgw = sb_tile("xgw", [P, J], U16)
+        nc.vector.tensor_copy(xgs[:], xs[:].indirect(l1[:]))
+        nc.vector.tensor_copy(xgw[:], xw[:].indirect(l1[:]))
+
+        def deal(name, words, plane):
+            dw = [sb_tile(f"{name}_dw{u}", [P, 2, P], U32) for u in range(2)]
+            ds = [sb_tile(f"{name}_ds{u}", [P, 2, P], U8) for u in range(2)]
+            by_slot = plane.rearrange("p (m t) -> p t m", t=PACK)
+            by_col = words[:].rearrange("p (m t) -> p m t", t=PACK)
+            for u in range(2):
+                nc.gpsimd.tensor_copy(ds[u][:], by_slot[:, 2 * u : 2 * u + 2, :])
+                nc.scalar.copy(dw[u][:].rearrange("p t m -> p m t"), by_col[:, :, 2 * u : 2 * u + 2])
+            return dw, ds
+
+        w2d, w2ds = deal("w2", w2w, w2s[:, 0, :])
+        wd, wds = deal("w", ww, ws[:])
+
+        def first(acc, dw, ds, fmt, t):
+            nc.tensor.matmul_mx(
+                out=acc, lhsT=dw[t // 2][:, t % 2, :].bitcast(fmt), lhsT_scale=ds[t // 2][:, t % 2, :],
+                rhs=xgw[:].bitcast(E2M1), rhs_scale=xgs[:], start=True, stop=True,
+            )
+
+        b_ps = [psum.tile([P, J], F32, name=f"b_ps{t}") for t in range(PACK)]
+        a_ps = [psum.tile([P, 2, J], F32, name=f"a_ps{u}") for u in range(2)]
+        b_sb = [sb_tile(f"b_sb{t}", [P, 2 * J], F32) for t in range(PACK)]
+        a_sb = [sb_tile(f"a_sb{t}", [P, J], F32) for t in range(PACK)]
+        gb = [sb_tile(f"gb{t}", [P, J], F32) for t in range(PACK)]
+        d1 = sb_tile("d1", [P, PACK, J], F32)
+
+        for t in range(PACK):
+            first(b_ps[t][:], w2d, w2ds, E4M3, t)
+            nc.vector.tensor_copy(b_sb[t][:, 0:J], b_ps[t][:])
+            nc.scalar.activation(out=gb[t][:], in_=b_sb[t][:].indirect(l2[:]), func=COPY, scale=sa_t[:, t : t + 1])
+        for u in range(2):
+            for t in (2 * u, 2 * u + 1):
+                first(a_ps[u][:, t % 2, :], wd, wds, E5M2, t)
+            for t in (2 * u, 2 * u + 1):
+                nc.vector.tensor_copy(a_sb[t][:], a_ps[u][:, t % 2, :])
+                nc.gpsimd.tensor_tensor(d1[:, t, :], a_sb[t][:], gb[t][:], SUB)
+
+        vgw = sb_tile("vgw", [P, N], U32)
+        vgs = sb_tile("vgs", [P, N], U8)
+        nc.vector.tensor_copy(vgw[:], vw[:].indirect(l4[:]))
+        nc.vector.tensor_copy(vgs[:], vs[:].indirect(l4[:]))
+
+        out_v = out.rearrange("(u p) j -> p u j", p=P)
+        for h in range(2):
+            cols = slice(h * HALF, (h + 1) * HALF)
+            d2 = sb_tile("d2", [P, PACK, HALF], F32)
+            for t in range(PACK):
+                ga = sb_tile(f"ga{h}_{t}", [P, HALF], F32)
+                nc.scalar.activation(
+                    out=ga[:], in_=a_sb[t][:].indirect(l3[:, h * 8 : (h + 1) * 8]), func=COPY, scale=sb_t[:, t : t + 1],
+                )
+                nc.vector.tensor_tensor(d2[:, t, :], b_ps[t][:, cols], ga[:], SUB)
+            hid = sb_tile(f"hid{h}", [P, HALF * PACK], BF16)
+            nc.vector.tensor_tensor(
+                hid[:].rearrange("p (c i t) -> p c t i", i=2, t=PACK),
+                d1[:, :, cols].rearrange("p t (c i) -> p c t i", i=2),
+                d2[:].rearrange("p t (c i) -> p c t i", i=2),
+                MAX,
+            )
+            hw = sb_tile(f"hw{h}", [P, HALF], U32)
+            hs = sb_tile(f"hs{h}", [P, HALF], U8)
+            nc.vector.quantize_mx(out=hw[:].bitcast(E5M2), scales=hs[:], in_=hid[:])
+            if h == 0:
+                y_all = psum.tile([P, 2, HALF], F32, name="y_ps0")
+                y_ps = [y_all[:, 0, :], y_all[:, 1, :]]
+            else:
+                y_two = [psum.tile([P, HALF], F32, name=f"y_ps1{u}", tag=f"a_ps{u}") for u in range(2)]
+                y_ps = [y_two[0][:], y_two[1][:]]
+            for u in range(2):
+                nc.tensor.matmul_mx(
+                    out=y_ps[u], lhsT=vgw[:, u * P : (u + 1) * P].bitcast(E4M3), lhsT_scale=vgs[:, u * P : (u + 1) * P],
+                    rhs=hw[:].bitcast(E5M2), rhs_scale=hs[:], start=True, stop=True,
+                )
+            if h == 0:
+                y_sb = sb_tile("y_sb0", [P, 2, HALF], F32)
+                nc.scalar.copy(y_sb[:], y_all[:])
+                nc.sync.dma_start(out_v[:, :, cols], y_sb[:])
+            else:
+                y_a = sb_tile("y_sb10", [P, HALF], F32)
+                y_b = sb_tile("y_sb11", [P, HALF], F32)
+                nc.scalar.copy(y_a[:], y_ps[0])
+                nc.scalar.dma_start(out_v[:, 0, cols], y_a[:])
+                nc.vector.tensor_copy(y_b[:], y_ps[1])
+                nc.sync.dma_start(out_v[:, 1, cols], y_b[:])

@@ -137,25 +137,37 @@ def tile_list_mutualweighed_twow_store_plain_kernel(
         nc.vector.tensor_copy(vgs[:], vs[:].indirect(l4[:]))
 
         out_v = out.rearrange("(u p) j -> p u j", p=P)
-        for h in range(2):
+        d2_all = sb_tile("d2", [P, PACK + 1, HALF], F32)
+        hid = [sb_tile(f"hid{h}", [P, HALF * PACK], BF16) for h in range(2)]
+
+        def second(h):
             cols = slice(h * HALF, (h + 1) * HALF)
-            d2 = sb_tile("d2", [P, PACK, HALF], F32)
             for t in range(PACK):
                 ga = sb_tile(f"ga{h}_{t}", [P, HALF], F32)
                 nc.scalar.activation(
                     out=ga[:], in_=a_sb[t][:].indirect(l3[:, h * 8 : (h + 1) * 8]), func=COPY, scale=sb_t[:, t : t + 1],
                 )
-                nc.vector.tensor_tensor(d2[:, t, :], b_ps[t][:, cols], ga[:], SUB)
-            hid = sb_tile(f"hid{h}", [P, HALF * PACK], BF16)
+                nc.vector.tensor_tensor(d2_all[:, t + 1 - h, :], b_ps[t][:, cols], ga[:], SUB)
+
+        def larger(h):
+            cols = slice(h * HALF, (h + 1) * HALF)
             nc.vector.tensor_tensor(
-                hid[:].rearrange("p (c i t) -> p c t i", i=2, t=PACK),
+                hid[h][:].rearrange("p (c i t) -> p c t i", i=2, t=PACK),
                 d1[:, :, cols].rearrange("p t (c i) -> p c t i", i=2),
-                d2[:].rearrange("p t (c i) -> p c t i", i=2),
+                d2_all[:, 1 - h : 1 - h + PACK, :].rearrange("p t (c i) -> p c t i", i=2),
                 MAX,
             )
+
+        second(0)
+        larger(0)
+        second(1)
+        for h in range(2):
+            cols = slice(h * HALF, (h + 1) * HALF)
+            if h == 1:
+                larger(1)
             hw = sb_tile(f"hw{h}", [P, HALF], U32)
             hs = sb_tile(f"hs{h}", [P, HALF], U8)
-            nc.vector.quantize_mx(out=hw[:].bitcast(E5M2), scales=hs[:], in_=hid[:])
+            nc.vector.quantize_mx(out=hw[:].bitcast(E5M2), scales=hs[:], in_=hid[h][:])
             if h == 0:
                 y_all = psum.tile([P, 2, HALF], F32, name="y_ps0")
                 y_ps = [y_all[:, 0, :], y_all[:, 1, :]]

from contextlib import ExitStack

import concourse.mybir as mybir

K, T, J, R, N, S = 512, 1024, 256, 512, 256, 1024
FLOPS = 2 * 2 * K * R * J + 2 * R * N * J

F32 = mybir.dt.float32
BF16 = mybir.dt.bfloat16
I32 = mybir.dt.int32
U32 = mybir.dt.uint32
U16 = mybir.dt.uint16
U8 = mybir.dt.uint8
E4M3 = mybir.dt.float8_e4m3fn_x4
E5M2 = mybir.dt.float8_e5m2_x4
E2M1 = mybir.dt.float4_e2m1fn_x4
COPY = mybir.ActivationFunctionType.Copy
SUB = mybir.AluOpType.subtract
MAX = mybir.AluOpType.max

P = 128
PACK = 4
HALF = J // 2
LIST_COLS = J // 16


def tile_list_mutualweighed_twow_store_plain_kernel(
    tc, xt_words, xt_scales, w_words, w_scales, w2_words, w2_scales, sa, sb, vs_words, vs_scales,
    offs, offs2, offs3, offs4, out,
):
    nc = tc.nc
    with ExitStack() as ctx:
        pool = ctx.enter_context(tc.tile_pool(name="held", bufs=1))
        psum = ctx.enter_context(tc.psum_pool(name="psum", bufs=1))

        def sb_tile(name, shape, dtype):
            return pool.tile(shape, dtype, name=name, align_bytes=64)

        def packed(words):
            return words[0].rearrange("p n t -> p (n t)").bitcast(I32)

        def load_two(queue, tile, scales):
            rows = scales[0].bitcast(I32).rearrange("(u v r) c -> v r u c", u=2, v=2)
            for v in range(2):
                queue.dma_start(tile[32 * v : 32 * v + 4].bitcast(I32), rows[v])

        def load_four(queue, tile, scales):
            rows = scales[0].bitcast(I32)
            for q in range(4):
                queue.dma_start(tile[32 * q : 32 * q + 4, :].bitcast(I32), rows[4 * q : 4 * q + 4, :])

        l1 = sb_tile("l1", [P, LIST_COLS], U16)
        l2 = sb_tile("l2", [P, LIST_COLS], U16)
        l3 = sb_tile("l3", [P, LIST_COLS], U16)
        l4 = sb_tile("l4", [P, LIST_COLS], U16)
        xw = sb_tile("xw", [P, T], U16)
        xs2 = sb_tile("xs2", [P, 2, T], U8)
        xs = sb_tile("xs", [P, T], U8)
        ww = sb_tile("ww", [P, R], U32)
        ws = sb_tile("ws", [P, R], U8)
        w2w = sb_tile("w2w", [P, R], U32)
        w2s = sb_tile("w2s", [P, 2, R], U8)
        vw = sb_tile("vw", [P, S], U32)
        vs = sb_tile("vs", [P, S], U8)
        sa_t = sb_tile("sa_t", [P, PACK], F32)
        sb_t = sb_tile("sb_t", [P, PACK], F32)

        nc.vector.memset(w2s[0:64].bitcast(I32), 0)
        nc.vector.memset(xs2[0:64, 0, :].bitcast(I32), 0)
        nc.gpsimd.memset(xs2[0:64, 1, :].bitcast(I32), 0)
        nc.gpsimd.memset(ws[:].bitcast(I32), 0)
        nc.gpsimd.memset(vs[:].bitcast(I32), 0)

        nc.sync.dma_start(l1[:], offs)
        nc.scalar.dma_start(xw[:].bitcast(I32), xt_words[0].bitcast(I32))
        load_two(nc.sync, w2s, w2_scales)
        load_two(nc.sync, xs2, xt_scales)
        nc.sync.dma_start(w2w[:].bitcast(I32), packed(w2_words))
        nc.sync.dma_start(ww[:].bitcast(I32), packed(w_words))
        nc.gpsimd.dma_start(sa_t[:], sa.rearrange("(p t) o -> p (t o)", t=PACK))
        nc.sync.dma_start(l2[:], offs2)
        load_four(nc.sync, ws, w_scales)
        nc.sync.dma_start(vw[:].bitcast(I32), packed(vs_words))
        nc.sync.dma_start(l4[:], offs4)
        load_four(nc.sync, vs, vs_scales)
        nc.sync.dma_start(sb_t[:], sb.rearrange("(p t) o -> p (t o)", t=PACK))
        nc.sync.dma_start(l3[:], offs3)

        nc.vector.tensor_copy(xs[0:64, :].bitcast(I32), xs2[0:64, 0, :].bitcast(I32))
        nc.vector.tensor_copy(xs[64:128, :].bitcast(I32), xs2[0:64, 1, :].bitcast(I32))
        nc.vector.tensor_copy(w2s[64:128, 0, :].bitcast(I32), w2s[0:64, 1, :].bitcast(I32))
        xgs = sb_tile("xgs", [P, J], U8)
        xgw = sb_tile("xgw", [P, J], U16)
        nc.vector.tensor_copy(xgs[:], xs[:].indirect(l1[:]))
        nc.vector.tensor_copy(xgw[:], xw[:].indirect(l1[:]))

        def deal(name, words, plane):
            dw = [sb_tile(f"{name}_dw{u}", [P, 2, P], U32) for u in range(2)]
            ds = [sb_tile(f"{name}_ds{u}", [P, 2, P], U8) for u in range(2)]
            by_slot = plane.rearrange("p (m t) -> p t m", t=PACK)
            by_col = words[:].rearrange("p (m t) -> p m t", t=PACK)
            for u in range(2):
                nc.gpsimd.tensor_copy(ds[u][:], by_slot[:, 2 * u : 2 * u + 2, :])
                nc.scalar.copy(dw[u][:].rearrange("p t m -> p m t"), by_col[:, :, 2 * u : 2 * u + 2])
            return dw, ds

        w2d, w2ds = deal("w2", w2w, w2s[:, 0, :])
        wd, wds = deal("w", ww, ws[:])

        def first(acc, dw, ds, fmt, t):
            nc.tensor.matmul_mx(
                out=acc, lhsT=dw[t // 2][:, t % 2, :].bitcast(fmt), lhsT_scale=ds[t // 2][:, t % 2, :],
                rhs=xgw[:].bitcast(E2M1), rhs_scale=xgs[:], start=True, stop=True,
            )

        b_ps = [psum.tile([P, J], F32, name=f"b_ps{t}") for t in range(PACK)]
        a_ps = [psum.tile([P, 2, J], F32, name=f"a_ps{u}") for u in range(2)]
        b_sb = [sb_tile(f"b_sb{t}", [P, 2 * J], F32) for t in range(PACK)]
        a_sb = [sb_tile(f"a_sb{t}", [P, J], F32) for t in range(PACK)]
        gb = [sb_tile(f"gb{t}", [P, J], F32) for t in range(PACK)]
        d1 = sb_tile("d1", [P, PACK, J], F32)

        for t in range(PACK):
            first(b_ps[t][:], w2d, w2ds, E4M3, t)
            nc.vector.tensor_copy(b_sb[t][:, 0:J], b_ps[t][:])
            nc.scalar.activation(out=gb[t][:], in_=b_sb[t][:].indirect(l2[:]), func=COPY, scale=sa_t[:, t : t + 1])
        for u in range(2):
            for t in (2 * u, 2 * u + 1):
                first(a_ps[u][:, t % 2, :], wd, wds, E5M2, t)
            for t in (2 * u, 2 * u + 1):
                nc.vector.tensor_copy(a_sb[t][:], a_ps[u][:, t % 2, :])
                nc.gpsimd.tensor_tensor(d1[:, t, :], a_sb[t][:], gb[t][:], SUB)

        vgw = sb_tile("vgw", [P, N], U32)
        vgs = sb_tile("vgs", [P, N], U8)
        nc.vector.tensor_copy(vgw[:], vw[:].indirect(l4[:]))
        nc.vector.tensor_copy(vgs[:], vs[:].indirect(l4[:]))

        out_v = out.rearrange("(u p) j -> p u j", p=P)
        d2_all = sb_tile("d2", [P, PACK + 1, HALF], F32)
        hid = [sb_tile(f"hid{h}", [P, HALF * PACK], BF16) for h in range(2)]

        def second(h):
            cols = slice(h * HALF, (h + 1) * HALF)
            for t in range(PACK):
                ga = sb_tile(f"ga{h}_{t}", [P, HALF], F32)
                nc.scalar.activation(
                    out=ga[:], in_=a_sb[t][:].indirect(l3[:, h * 8 : (h + 1) * 8]), func=COPY, scale=sb_t[:, t : t + 1],
                )
                nc.vector.tensor_tensor(d2_all[:, t + 1 - h, :], b_ps[t][:, cols], ga[:], SUB)

        def larger(h):
            cols = slice(h * HALF, (h + 1) * HALF)
            nc.vector.tensor_tensor(
                hid[h][:].rearrange("p (c i t) -> p c t i", i=2, t=PACK),
                d1[:, :, cols].rearrange("p t (c i) -> p c t i", i=2),
                d2_all[:, 1 - h : 1 - h + PACK, :].rearrange("p t (c i) -> p c t i", i=2),
                MAX,
            )

        second(0)
        larger(0)
        second(1)
        for h in range(2):
            cols = slice(h * HALF, (h + 1) * HALF)
            if h == 1:
                larger(1)
            hw = sb_tile(f"hw{h}", [P, HALF], U32)
            hs = sb_tile(f"hs{h}", [P, HALF], U8)
            nc.vector.quantize_mx(out=hw[:].bitcast(E5M2), scales=hs[:], in_=hid[h][:])
            if h == 0:
                y_all = psum.tile([P, 2, HALF], F32, name="y_ps0")
                y_ps = [y_all[:, 0, :], y_all[:, 1, :]]
            else:
                y_two = [psum.tile([P, HALF], F32, name=f"y_ps1{u}", tag=f"a_ps{u}") for u in range(2)]
                y_ps = [y_two[0][:], y_two[1][:]]
            for u in range(2):
                nc.tensor.matmul_mx(
                    out=y_ps[u], lhsT=vgw[:, u * P : (u + 1) * P].bitcast(E4M3), lhsT_scale=vgs[:, u * P : (u + 1) * P],
                    rhs=hw[:].bitcast(E5M2), rhs_scale=hs[:], start=True, stop=True,
                )
            if h == 0:
                y_sb = sb_tile("y_sb0", [P, 2, HALF], F32)
                nc.scalar.copy(y_sb[:], y_all[:])
                nc.sync.dma_start(out_v[:, :, cols], y_sb[:])
            else:
                y_a = sb_tile("y_sb10", [P, HALF], F32)
                y_b = sb_tile("y_sb11", [P, HALF], F32)
                nc.scalar.copy(y_a[:], y_ps[0])
                nc.scalar.dma_start(out_v[:, 0, cols], y_a[:])
                nc.vector.tensor_copy(y_b[:], y_ps[1])
                nc.sync.dma_start(out_v[:, 1, cols], y_b[:])
